import numpy as np, ml_dtypes
CORES = [33,161,289,417,57,185,313,441]
N = 8
KB, QP = 1, 32
MEM = [5,6]
def setup_inputs(rng):
    q = rng.standard_normal((N, 128, QP), dtype=np.float32) / 4; k = rng.standard_normal((N, 128, KB * 128), dtype=np.float32)
    a = 2 * np.pi * rng.random((N, QP)); s = 400 * rng.random((N, QP)) ** 1.5; q[:, 0, :] = s * np.cos(a); q[:, 1, :] = s * np.sin(a); q[:, 2, :] = 150 * rng.standard_normal((N, QP)); k[:, 2, :] = 1 + k[:, 2, :] / 50
    c = np.zeros(N); c[MEM] = rng.permutation(len(MEM))
    a = (2 * np.pi * rng.random() + np.pi / 2 * (c.reshape(N, 1, 1) + 0.5) / len(MEM) - 0.5 + (np.arange(KB).reshape(1, KB, 1) + rng.random((N, KB, 128))) / KB).reshape(N, KB * 128); k[:, 0, :] = np.cos(a); k[:, 1, :] = np.sin(a)
    return {"q": q.astype(ml_dtypes.bfloat16), "k": k.astype(ml_dtypes.bfloat16), "v": rng.standard_normal((N, 128, KB * 128), dtype=np.float32).astype(ml_dtypes.bfloat16)}
def setup_inputs_big(rng):
    d = setup_inputs(rng)
    for k in ("v",): d[k] = (d[k].astype(np.float32) * 1048576.0).astype(d[k].dtype)
    return d
def setup_inputs_small(rng):
    d = setup_inputs(rng)
    for k in ("v",): d[k] = (d[k].astype(np.float32) * (1 / 1048576.0)).astype(d[k].dtype)
    return d
def reference(q, k, v):
    Q, K, V = q.astype(np.float64), k.astype(np.float64), v.astype(np.float64)
    y = np.zeros((N, QP, 128))
    for r in range(N):
        js = list(MEM)
        S = np.concatenate([K[j].T @ Q[r] for j in js], axis=0)
        P = np.exp(S - S.max(axis=0)); P = P / P.sum(axis=0)
        y[r] = P.T @ np.concatenate([V[j][:, 128 * b:128 * b + 128] for j in js for b in range(KB)], axis=0)
    return {"y": y.astype(ml_dtypes.bfloat16)}

from concourse.bass import DstId, RemoteDMATransfer
from concourse.mybir import AluOpType, AxisListType, ActivationFunctionType

WORLD = 512
QP = 32

SCRATCH = {
    "kd": ("dram", [128, 128], "bfloat16"),
    "vd": ("dram", [128, 128], "bfloat16"),
    "stage": ("dram", [128, 128], "bfloat16"),
    "KV": ("sbuf", [128, 512], "bfloat16"),
    "qs": ("sbuf", [128, QP], "bfloat16"),
    "msk": ("sbuf", [128, QP], "float32"),
    "ident": ("sbuf", [128, QP], "bfloat16"),
    "negm": ("sbuf", [128, 4], "float32"),
    "lsum": ("sbuf", [128, 4], "float32"),
    "rinv": ("sbuf", [128, 4], "float32"),
    "P": ("sbuf", [128, 256], "bfloat16"),
    "PT": ("sbuf", [128, 2 * QP], "bfloat16"),
    "ysb": ("sbuf", [128, 128], "bfloat16"),
    "psS": ("psum", [128, 512], "float32"),
    "psT": ("psum", [128, 1024], "bfloat16"),
    "psO": ("psum", [128, 512], "float32"),
}
SEMAPHORES = ["ldd", "lds", "stg", "snt", "tk0", "tv0", "tk1", "tv1",
              "c_z", "c_a", "c_i", "c_s", "c_m", "c_p", "c_t", "c_c", "c_o", "c_r", "c_y", "st"]

_CACHE = {}


def _bits(mask):
    return [b for b in range(16) if (mask >> b) & 1]


def _mk(bits):
    m = 0
    for b in bits:
        m |= 1 << b
    return m


def make_plan(cores, mem, topo):
    src = [cores[m] for m in mem]

    def helpers(c):
        return [d for d in range(WORLD) if topo.host(d) == topo.host(c) and topo.chip(d) == topo.chip(c)
                and d not in cores]

    def group(x):
        return [c for c in cores if c != x and topo.rack(topo.host(c)) == topo.rack(topo.host(x))]

    far = [[c for c in group(x) if not topo.may_write(x, c)] for x in src]
    near = [[c for c in group(x) if topo.may_write(x, c)] for x in src]
    relay, first, direct = {}, [{"k": [], "v": []}, {"k": [], "v": []}], [[], []]
    own = [{}, {}]
    for j in (0, 1):
        x, y = src[j], src[1 - j]
        owners = [h for h in helpers(x) if all(topo.may_write(h, f) for f in far[j])]
        same = [h for h in owners if topo.die(h) == topo.die(y)]
        oth = [h for h in owners if topo.die(h) != topo.die(y)]
        relay[same[0]] = (1 - j, "k", far[j])
        relay[oth[0]] = (1 - j, "v", far[j])
        relay[same[1]] = (j, "k", far[j])
        relay[oth[1]] = (j, "v", far[j])
        first[1 - j]["k"].append(same[0])
        first[1 - j]["v"].append(oth[0])
        own[j] = {"k": same[1], "v": oth[1]}
    for j in (0, 1):
        x, y = src[j], src[1 - j]
        first[j]["k"].append(own[j]["k"])
        first[j]["v"].append(own[j]["v"])
        direct[j] = [y] + near[j]
        lost = [c for c in near[1 - j] if not topo.may_write(x, c)]
        if lost:
            hs = [h for h in helpers(near[j][0]) if topo.may_write(x, h) and all(topo.may_write(h, c) for c in lost)]
            ok = [h for h in hs if topo.die(h) == topo.die(x)][0]
            ov = [h for h in hs if topo.die(h) != topo.die(x)][0]
            relay[ok] = (j, "k", lost)
            relay[ov] = (j, "v", lost)
            first[j]["k"].append(ok)
            first[j]["v"].append(ov)
    return {"src": src, "relay": relay, "first": first, "direct": direct}


def _col(j, kind):
    return 256 * j + (0 if kind == "k" else 128)


def _send(g, T, topo, core, src_ap, dst_fn, dests, bits, sem):
    ids = []
    for d in dests:
        rid, pid = topo.addr(d, core)
        ids.append(DstId(rid=rid, pnc=pid))
    return RemoteDMATransfer(dst_ids=ids, dma_engine_mask=_mk(bits), remote_sem=sem,
                             srcs=[src_ap], dsts=[dst_fn() for _ in dests], alu_op=0)


def _common_bits(topo, core, dests):
    m = topo.mask(core, dests[0])
    for d in dests[1:]:
        m &= topo.mask(core, d)
    return _bits(m)


def rank_program(g, core, T, topo):
    if "plan" not in _CACHE:
        _CACHE["plan"] = make_plan(list(T.cores), list(T.tables["MEM"]), topo)
    plan = _CACHE["plan"]
    src, relay, first, direct = plan["src"], plan["relay"], plan["first"], plan["direct"]
    S = T.sem

    if core in relay:
        j, kind, dests = relay[core]
        x = src[j]
        n_in = len(_common_bits(topo, x, first[j]["k"] + first[j]["v"])) // 2
        bits = _common_bits(topo, core, dests)
        c0 = _col(j, kind)
        g.wait_ge(S.stg, n_in)
        g.remote_dma_fused([_send(g, T, topo, core, T.stage[:, :], lambda: T.KV[:, c0:c0 + 128], dests, bits,
                                  S["t%s%d" % (kind, j)])], local_sem=S.snt)
        g.wait_ge(S.snt, len(bits))
        return

    rank = T.rank_of(core)
    if rank is None:
        return
    me = src.index(core) if core in src else None

    n_lds = 16
    if me is not None:
        ck, cv = _col(me, "k"), _col(me, "v")
        g.sync.dma_start(T.kd[:, :], T.k[:, :]).then_inc(S.ldd, 16)
        g.scalar.dma_start(T.vd[:, :], T.v[:, :]).then_inc(S.ldd, 16)
        g.sync.dma_start(T.KV[:, ck:ck + 128], T.k[:, :]).then_inc(S.lds, 16)
        g.scalar.dma_start(T.KV[:, cv:cv + 128], T.v[:, :]).then_inc(S.lds, 16)
        n_lds = 48
    g.sync.dma_start(T.qs[:, :], T.q[:, :]).then_inc(S.lds, 16)

    g.vector.memset(T.msk[0:QP, :], 0.0).then_inc(S.c_z, 1)
    g.wait_ge(S.c_z, 1)
    g.affine_select(T.msk[0:QP, :], T.msk[0:QP, :], [[-1, QP]], AluOpType.is_equal, -30000.0, 0, 1).then_inc(S.c_a, 1)
    g.scalar.wait_ge(S.c_a, 1)
    g.scalar.activation(T.ident[0:QP, :], T.msk[0:QP, :], ActivationFunctionType.Exp).then_inc(S.c_i, 1)

    if me is not None:
        bits = _common_bits(topo, core, first[me]["k"] + first[me]["v"])
        h = len(bits) // 2
        g.wait_ge(S.ldd, 32)
        g.remote_dma_fused([
            _send(g, T, topo, core, T.kd[:, :], lambda: T.stage[:, :], first[me]["k"], bits[:h], S.stg),
            _send(g, T, topo, core, T.vd[:, :], lambda: T.stage[:, :], first[me]["v"], bits[h:2 * h], S.stg),
        ], local_sem=S.snt)
        dbits = _common_bits(topo, core, direct[me])
        c0 = _col(me, "k")
        g.wait_ge(S.lds, n_lds)
        g.remote_dma_fused([_send(g, T, topo, core, T.KV[:, c0:c0 + 256], lambda: T.KV[:, c0:c0 + 256], direct[me],
                                  dbits, S["tk%d" % me])], local_sem=S.snt)
        g.wait_ge(S.snt, 2 * h + len(dbits))

    def tile_wait(j, kind):
        if core == src[j]:
            return S.lds, n_lds
        if core in direct[j]:
            return S["tk%d" % j], len(_common_bits(topo, src[j], direct[j]))
        r = [c for c in relay if relay[c][0] == j and relay[c][1] == kind and core in relay[c][2]][0]
        return S["t%s%d" % (kind, j)], len(_common_bits(topo, r, relay[r][2]))

    early = [j for j in (0, 1) if topo.rack(topo.host(src[j])) == topo.rack(topo.host(core))][0]
    order = [early, 1 - early]
    pe, dve, act = g.tensor, g.vector, g.scalar

    pe.wait_ge(S.lds, n_lds)
    for j in order:
        s, n = tile_wait(j, "k")
        pe.wait_ge(s, n)
        pe.matmul(T.psS[0:QP, 128 * j:128 * j + 128], T.qs[:, :], T.KV[:, _col(j, "k"):_col(j, "k") + 128],
                  True, True).then_inc(S.c_s, 1)
    dve.wait_ge(S.c_s, 2)
    dve.tensor_reduce(T.negm[0:QP, 0:1], T.psS[0:QP, 0:256], AxisListType.X, AluOpType.max,
                      negate=True).then_inc(S.c_m, 1)
    act.wait_ge(S.c_m, 1)
    act.activation(T.P[0:QP, :], T.psS[0:QP, 0:256], ActivationFunctionType.Exp, bias=T.negm[0:QP, 0:1], scale=1.0,
                   accum_out=T.lsum[0:QP, 0:1]).then_inc(S.c_p, 1)
    pe.wait_ge(S.c_i, 1)
    pe.wait_ge(S.c_p, 1)
    for j in (0, 1):
        pe.transpose(T.psT[:, QP * j:QP * j + QP], T.P[0:QP, 128 * j:128 * j + 128],
                     T.ident[0:QP, :]).then_inc(S.c_t, 1)
    dve.wait_ge(S.c_t, 2)
    dve.tensor_copy(T.PT[:, :], T.psT[:, 0:2 * QP]).then_inc(S.c_c, 1)
    dve.wait_ge(S.c_p, 1)
    dve.reciprocal(T.rinv[0:QP, 0:1], T.lsum[0:QP, 0:1]).then_inc(S.c_r, 1)
    pe.wait_ge(S.c_c, 1)
    for i, j in enumerate(order):
        s, n = tile_wait(j, "v")
        pe.wait_ge(s, n)
        mm = pe.matmul(T.psO[0:QP, 0:128], T.PT[:, QP * j:QP * j + QP], T.KV[:, _col(j, "v"):_col(j, "v") + 128],
                       i == 0, i == 1)
    mm.then_inc(S.c_o, 1)
    dve.wait_ge(S.c_o, 1)
    dve.wait_ge(S.c_r, 1)
    dve.tensor_scalar(T.ysb[0:QP, :], T.psO[0:QP, 0:128], T.rinv[0:QP, 0:1], None, AluOpType.mult).then_inc(S.c_y, 1)
    g.sync.wait_ge(S.c_y, 1)
    g.sync.dma_start(T.y[:, :], T.ysb[0:QP, :]).then_inc(S.st, 16)
    g.sync.wait_ge(S.st, 16)
